import numpy as np, ml_dtypes
CORES = [30,158,46,174,86,214]
N = 6
NP, TK = 2, 128
def setup_inputs(rng):
    return {"x": rng.standard_normal((N, 128, TK), dtype=np.float32).astype(ml_dtypes.bfloat16), "w1": (rng.standard_normal((N, 128, 128), dtype=np.float32) / 8).astype(ml_dtypes.bfloat16), "w2": (rng.standard_normal((N, 128, NP * 128), dtype=np.float32) / 8).astype(ml_dtypes.bfloat16)}
def setup_inputs_big(rng):
    d = setup_inputs(rng)
    for k in ("x", "w1", "w2"): d[k] = (d[k].astype(np.float32) * 1024.0).astype(d[k].dtype)
    return d
def setup_inputs_small(rng):
    d = setup_inputs(rng)
    for k in ("x", "w1", "w2"): d[k] = (d[k].astype(np.float32) * (1 / 1024.0)).astype(d[k].dtype)
    return d
def setup_inputs_apart(rng):
    d = setup_inputs(rng)
    f = (10.0 ** rng.permutation(np.linspace(-1.5, 1.5, N))).astype(np.float32).reshape(N, 1, 1)
    for k in ("x", "w1", "w2"): d[k] = (d[k].astype(np.float32) * f).astype(d[k].dtype)
    return d
def reference(x, w1, w2):
    X, W1, W2 = x.astype(np.float64), w1.astype(np.float64), w2.astype(np.float64)
    h = [np.maximum(W1[p].T @ X[p], 0.0) for p in range(NP)]
    y = np.full((N, 128, TK), np.nan)
    for q in range(NP, N):
        y[q] = sum(W2[q][:, 128 * p:128 * p + 128].T @ h[p] for p in range(NP))
    return {"y": y.astype(ml_dtypes.bfloat16 if x.dtype != np.float64 else np.float64)}

@@ -1,0 +1,97 @@
+from concourse.bass import DstId, RemoteDMATransfer
+from concourse.mybir import AluOpType
+
+NP = 2
+TK = 128
+
+SCRATCH = {
+    "xs": ("sbuf", [128, TK], "bfloat16"),
+    "w1s": ("sbuf", [128, 128], "bfloat16"),
+    "zero": ("sbuf", [128, TK], "float32"),
+    "h": ("sbuf", [128, TK], "bfloat16"),
+    "w2s": ("sbuf", [128, NP * 128], "bfloat16"),
+    "land0": ("sbuf", [128, TK], "bfloat16"),
+    "land1": ("sbuf", [128, TK], "bfloat16"),
+    "ys": ("sbuf", [128, TK], "bfloat16"),
+    "acc": ("psum", [128, TK], "float32"),
+}
+SEMAPHORES = ["ld", "zr", "mm", "ev", "sent", "arr0", "arr1", "st"]
+
+
+def _engines(mask):
+    return [1 << b for b in range(mask.bit_length()) if (mask >> b) & 1]
+
+
+def _producer(g, core, T, topo, p):
+    S = T.sem
+    g.sync.dma_start(T.w1s[:], T.w1[:]).then_inc(S.ld, 16)
+    g.scalar.dma_start(T.xs[:], T.x[:]).then_inc(S.ld, 16)
+    g.vector.memset(T.zero[:], 0.0).then_inc(S.zr, 1)
+
+    g.tensor.wait_ge(S.ld, 32)
+    g.tensor.matmul(T.acc[:], T.w1s[:], T.xs[:], True, True).then_inc(S.mm, 1)
+
+    g.vector.wait_ge(S.zr, 1)
+    g.vector.wait_ge(S.mm, 1)
+    g.vector.tensor_tensor(T.h[:], T.acc[:], T.zero[:], AluOpType.max).then_inc(S.ev, 1)
+
+    dsts = list(T.cores[NP:])
+    allowed = topo.mask(core, dsts[0])
+    for d in dsts:
+        assert topo.may_write(core, d)
+        allowed &= topo.mask(core, d)
+    eng = _engines(allowed)
+    share = 1
+    while share * 2 * len(dsts) <= len(eng):
+        share *= 2
+    transfers = []
+    for k, d in enumerate(dsts):
+        rid, pid = topo.addr(d, core)
+        transfers.append(RemoteDMATransfer(
+            dst_ids=[DstId(rid=rid, pnc=pid)], dma_engine_mask=sum(eng[k * share:(k + 1) * share]),
+            remote_sem=S["arr%d" % p], src=T.h[:], dst=T["land%d" % p][:]))
+    g.wait_ge(S.ev, 1)
+    g.remote_dma_fused(transfers, local_sem=S.sent)
+    g.wait_ge(S.sent, share * len(dsts))
+    return share
+
+
+def _share(core, T, topo):
+    src = T.cores[0]
+    dsts = list(T.cores[NP:])
+    allowed = topo.mask(src, dsts[0])
+    for d in dsts:
+        allowed &= topo.mask(src, d)
+    share = 1
+    while share * 2 * len(dsts) <= len(_engines(allowed)):
+        share *= 2
+    return share
+
+
+def _consumer(g, core, T, topo):
+    S = T.sem
+    n = _share(core, T, topo)
+    g.sync.dma_start(T.w2s[:], T.w2[:]).then_inc(S.ld, 16)
+
+    g.tensor.wait_ge(S.ld, 16)
+    for p in range(NP):
+        g.tensor.wait_ge(S["arr%d" % p], n)
+        mm = g.tensor.matmul(T.acc[:], T.w2s[:, 128 * p:128 * (p + 1)], T["land%d" % p][:], p == 0, p == NP - 1)
+    mm.then_inc(S.mm, 1)
+
+    g.vector.wait_ge(S.mm, 1)
+    g.vector.tensor_copy(T.ys[:], T.acc[:]).then_inc(S.ev, 1)
+
+    g.sync.wait_ge(S.ev, 1)
+    g.sync.dma_start(T.y[:], T.ys[:]).then_inc(S.st, 16)
+    g.sync.wait_ge(S.st, 16)
+
+
+def rank_program(g, core, T, topo):
+    rank = T.rank_of(core)
+    if rank is None:
+        return
+    if rank < NP:
+        _producer(g, core, T, topo, rank)
+    else:
+        _consumer(g, core, T, topo)

@@ -3,23 +3,44 @@ from concourse.mybir import AluOpType
 
 NP = 2
 TK = 128
+HALF = TK // 2
+BANK = 512
 
 SCRATCH = {
     "xs": ("sbuf", [128, TK], "bfloat16"),
     "w1s": ("sbuf", [128, 128], "bfloat16"),
-    "zero": ("sbuf", [128, TK], "float32"),
+    "zero": ("sbuf", [128, HALF], "float32"),
     "h": ("sbuf", [128, TK], "bfloat16"),
     "w2s": ("sbuf", [128, NP * 128], "bfloat16"),
     "land0": ("sbuf", [128, TK], "bfloat16"),
     "land1": ("sbuf", [128, TK], "bfloat16"),
     "ys": ("sbuf", [128, TK], "bfloat16"),
-    "acc": ("psum", [128, TK], "float32"),
+    "acc0": ("psum", [128, BANK], "float32"),
+    "acc1": ("psum", [128, BANK], "float32"),
 }
-SEMAPHORES = ["ld", "zr", "mm", "ev", "sent", "arr0", "arr1", "st"]
+SEMAPHORES = ["ld", "zr", "mm0", "mm1", "ev", "sent", "arr0", "arr1", "st"]
 
 
 def _engines(mask):
     return [1 << b for b in range(mask.bit_length()) if (mask >> b) & 1]
+
+
+def _lanes(T, topo, p):
+    src = T.cores[p]
+    kinds = [[d for d in T.cores[NP:] if not topo.same_plane(src, d)],
+             [d for d in T.cores[NP:] if topo.same_plane(src, d)]]
+    kinds = [k for k in kinds if k]
+    allowed = topo.mask(src, T.cores[NP])
+    for d in T.cores[NP:]:
+        assert topo.may_write(src, d)
+        allowed &= topo.mask(src, d)
+    eng = _engines(allowed)
+    lanes = []
+    for j, kind in enumerate(kinds):
+        r = p % len(kind)
+        mine = eng[j::len(kinds)]
+        lanes.append((kind[r:] + kind[:r], sum(mine), len(mine)))
+    return lanes
 
 
 def _producer(g, core, T, topo, p):
@@ -29,60 +50,53 @@ def _producer(g, core, T, topo, p):
     g.vector.memset(T.zero[:], 0.0).then_inc(S.zr, 1)
 
     g.tensor.wait_ge(S.ld, 32)
-    g.tensor.matmul(T.acc[:], T.w1s[:], T.xs[:], True, True).then_inc(S.mm, 1)
-
     g.vector.wait_ge(S.zr, 1)
-    g.vector.wait_ge(S.mm, 1)
-    g.vector.tensor_tensor(T.h[:], T.acc[:], T.zero[:], AluOpType.max).then_inc(S.ev, 1)
+    for c in range(2):
+        cols = slice(c * HALF, (c + 1) * HALF)
+        acc = T["acc%d" % c][:, 0:HALF]
+        g.tensor.matmul(acc, T.w1s[:], T.xs[:, cols], True, True).then_inc(S["mm%d" % c], 1)
+        g.vector.wait_ge(S["mm%d" % c], 1)
+        g.vector.tensor_tensor(T.h[:, cols], acc, T.zero[:], AluOpType.max).then_inc(S.ev, 1)
 
-    dsts = list(T.cores[NP:])
-    allowed = topo.mask(core, dsts[0])
-    for d in dsts:
-        assert topo.may_write(core, d)
-        allowed &= topo.mask(core, d)
-    eng = _engines(allowed)
-    share = 1
-    while share * 2 * len(dsts) <= len(eng):
-        share *= 2
-    transfers = []
-    for k, d in enumerate(dsts):
-        rid, pid = topo.addr(d, core)
-        transfers.append(RemoteDMATransfer(
-            dst_ids=[DstId(rid=rid, pnc=pid)], dma_engine_mask=sum(eng[k * share:(k + 1) * share]),
-            remote_sem=S["arr%d" % p], src=T.h[:], dst=T["land%d" % p][:]))
-    g.wait_ge(S.ev, 1)
-    g.remote_dma_fused(transfers, local_sem=S.sent)
-    g.wait_ge(S.sent, share * len(dsts))
-    return share
-
-
-def _share(core, T, topo):
-    src = T.cores[0]
-    dsts = list(T.cores[NP:])
-    allowed = topo.mask(src, dsts[0])
-    for d in dsts:
-        allowed &= topo.mask(src, d)
-    share = 1
-    while share * 2 * len(dsts) <= len(_engines(allowed)):
-        share *= 2
-    return share
+    g.wait_ge(S.ev, 2)
+    total = 0
+    for order, mask, n in _lanes(T, topo, p):
+        ids = []
+        for d in order:
+            rid, pid = topo.addr(d, core)
+            ids.append(DstId(rid=rid, pnc=pid))
+        g.remote_dma_fused([RemoteDMATransfer(
+            dst_ids=ids, dma_engine_mask=mask, remote_sem=S["arr%d" % p],
+            srcs=[T.h[:]], dsts=[T["land%d" % p][:] for _ in order])], local_sem=S.sent)
+        total += n
+    g.wait_ge(S.sent, total)
 
 
 def _consumer(g, core, T, topo):
     S = T.sem
-    n = _share(core, T, topo)
     g.sync.dma_start(T.w2s[:], T.w2[:]).then_inc(S.ld, 16)
 
-    g.tensor.wait_ge(S.ld, 16)
+    place, adds = {}, {}
     for p in range(NP):
-        g.tensor.wait_ge(S["arr%d" % p], n)
-        mm = g.tensor.matmul(T.acc[:], T.w2s[:, 128 * p:128 * (p + 1)], T["land%d" % p][:], p == 0, p == NP - 1)
-    mm.then_inc(S.mm, 1)
+        for order, mask, n in _lanes(T, topo, p):
+            if core in order:
+                place[p], adds[p] = order.index(core), n
+    turn = sorted(range(NP), key=lambda p: place[p])
 
-    g.vector.wait_ge(S.mm, 1)
-    g.vector.tensor_copy(T.ys[:], T.acc[:]).then_inc(S.ev, 1)
+    g.tensor.wait_ge(S.ld, 16)
+    for i, p in enumerate(turn):
+        g.tensor.wait_ge(S["arr%d" % p], adds[p])
+        for c in range(2):
+            mm = g.tensor.matmul(T["acc%d" % c][:, 0:HALF], T.w2s[:, 128 * p:128 * (p + 1)],
+                                 T["land%d" % p][:, c * HALF:(c + 1) * HALF], i == 0, i == NP - 1)
+            if i == NP - 1:
+                mm.then_inc(S["mm%d" % c], 1)
 
-    g.sync.wait_ge(S.ev, 1)
+    for c in range(2):
+        g.vector.wait_ge(S["mm%d" % c], 1)
+        g.vector.tensor_copy(T.ys[:, c * HALF:(c + 1) * HALF], T["acc%d" % c][:, 0:HALF]).then_inc(S.ev, 1)
+
+    g.sync.wait_ge(S.ev, 2)
     g.sync.dma_start(T.y[:], T.ys[:]).then_inc(S.st, 16)
     g.sync.wait_ge(S.st, 16)
 

from concourse.bass import DstId, RemoteDMATransfer
from concourse.mybir import AluOpType

NP = 2
TK = 128
HALF = TK // 2
BANK = 512

SCRATCH = {
    "xs": ("sbuf", [128, TK], "bfloat16"),
    "w1s": ("sbuf", [128, 128], "bfloat16"),
    "zero": ("sbuf", [128, HALF], "float32"),
    "h": ("sbuf", [128, TK], "bfloat16"),
    "w2s": ("sbuf", [128, NP * 128], "bfloat16"),
    "land0": ("sbuf", [128, TK], "bfloat16"),
    "land1": ("sbuf", [128, TK], "bfloat16"),
    "ys": ("sbuf", [128, TK], "bfloat16"),
    "acc0": ("psum", [128, BANK], "float32"),
    "acc1": ("psum", [128, BANK], "float32"),
}
SEMAPHORES = ["ld", "zr", "mm0", "mm1", "ev", "sent", "arr0", "arr1", "st"]


def _engines(mask):
    return [1 << b for b in range(mask.bit_length()) if (mask >> b) & 1]


def _lanes(T, topo, p):
    src = T.cores[p]
    kinds = [[d for d in T.cores[NP:] if not topo.same_plane(src, d)],
             [d for d in T.cores[NP:] if topo.same_plane(src, d)]]
    kinds = [k for k in kinds if k]
    allowed = topo.mask(src, T.cores[NP])
    for d in T.cores[NP:]:
        assert topo.may_write(src, d)
        allowed &= topo.mask(src, d)
    eng = _engines(allowed)
    lanes = []
    for j, kind in enumerate(kinds):
        r = p % len(kind)
        mine = eng[j::len(kinds)]
        lanes.append((kind[r:] + kind[:r], sum(mine), len(mine)))
    return lanes


def _producer(g, core, T, topo, p):
    S = T.sem
    g.sync.dma_start(T.w1s[:], T.w1[:]).then_inc(S.ld, 16)
    g.scalar.dma_start(T.xs[:], T.x[:]).then_inc(S.ld, 16)
    g.vector.memset(T.zero[:], 0.0).then_inc(S.zr, 1)

    g.tensor.wait_ge(S.ld, 32)
    g.vector.wait_ge(S.zr, 1)
    for c in range(2):
        cols = slice(c * HALF, (c + 1) * HALF)
        acc = T["acc%d" % c][:, 0:HALF]
        g.tensor.matmul(acc, T.w1s[:], T.xs[:, cols], True, True).then_inc(S["mm%d" % c], 1)
        g.vector.wait_ge(S["mm%d" % c], 1)
        g.vector.tensor_tensor(T.h[:, cols], acc, T.zero[:], AluOpType.max).then_inc(S.ev, 1)

    g.wait_ge(S.ev, 2)
    total = 0
    for order, mask, n in _lanes(T, topo, p):
        ids = []
        for d in order:
            rid, pid = topo.addr(d, core)
            ids.append(DstId(rid=rid, pnc=pid))
        g.remote_dma_fused([RemoteDMATransfer(
            dst_ids=ids, dma_engine_mask=mask, remote_sem=S["arr%d" % p],
            srcs=[T.h[:]], dsts=[T["land%d" % p][:] for _ in order])], local_sem=S.sent)
        total += n
    g.wait_ge(S.sent, total)


def _consumer(g, core, T, topo):
    S = T.sem
    g.sync.dma_start(T.w2s[:], T.w2[:]).then_inc(S.ld, 16)

    place, adds = {}, {}
    for p in range(NP):
        for order, mask, n in _lanes(T, topo, p):
            if core in order:
                place[p], adds[p] = order.index(core), n
    turn = sorted(range(NP), key=lambda p: place[p])

    g.tensor.wait_ge(S.ld, 16)
    for i, p in enumerate(turn):
        g.tensor.wait_ge(S["arr%d" % p], adds[p])
        for c in range(2):
            mm = g.tensor.matmul(T["acc%d" % c][:, 0:HALF], T.w2s[:, 128 * p:128 * (p + 1)],
                                 T["land%d" % p][:, c * HALF:(c + 1) * HALF], i == 0, i == NP - 1)
            if i == NP - 1:
                mm.then_inc(S["mm%d" % c], 1)

    for c in range(2):
        g.vector.wait_ge(S["mm%d" % c], 1)
        g.vector.tensor_copy(T.ys[:, c * HALF:(c + 1) * HALF], T["acc%d" % c][:, 0:HALF]).then_inc(S.ev, 1)

    g.sync.wait_ge(S.ev, 2)
    g.sync.dma_start(T.y[:], T.ys[:]).then_inc(S.st, 16)
    g.sync.wait_ge(S.st, 16)


def rank_program(g, core, T, topo):
    rank = T.rank_of(core)
    if rank is None:
        return
    if rank < NP:
        _producer(g, core, T, topo, rank)
    else:
        _consumer(g, core, T, topo)
